import numpy as np
import ml_dtypes


def mxq(x, axis, fmt="e4m3"):
    dtype, down = {"e4m3": (ml_dtypes.float8_e4m3fn, 7), "e5m2": (ml_dtypes.float8_e5m2, 14)}[fmt]
    v = np.moveaxis(np.asarray(x, np.float32).astype(ml_dtypes.bfloat16).astype(np.float64), axis, -1)
    blocks = v.reshape(v.shape[:-1] + (-1, 32))
    amax = np.abs(blocks).max(-1, keepdims=True)
    byte = np.maximum(np.where(amax > 0, np.frexp(amax)[1] - 1 + 127, 0) - down, 1)
    scale = np.exp2(byte - 127.0)
    codes = (blocks / scale).astype(np.float32).astype(dtype).astype(np.float64)
    return np.moveaxis((codes * scale).reshape(v.shape), -1, axis)


WIDE = False


def mx_kscale(k):
    if not WIDE:
        return np.ones(k)
    levels = np.array([10, -10, 5, -5, 0])
    if k % 512:
        return np.exp2(np.random.permutation(np.resize(levels, k // 32))).repeat(32)
    a = np.empty((k // 512, 16))
    for p in range(k // 512):
        a[p, :8] = np.random.permutation(np.resize(levels, 8))
        for g in range(8):
            far = levels[np.abs(levels - a[p, g]) >= 10]
            a[p, g + 8] = far[np.random.randint(len(far))]
    return np.exp2(a.ravel()).repeat(32)


def f64(x):
    return np.asarray(x).astype(np.float64)


def striped(idx):
    return np.tile(idx.reshape(-1, 16).T, (8, 1)).astype(np.uint16)


def unstriped(offs):
    return offs[:16].T.reshape(-1).astype(np.int64)


def striped8(idx):
    return np.concatenate([x.reshape(-1, 16).T for x in idx]).astype(np.uint16)


def runs(offs, k):
    lists = np.stack([offs[16 * r : 16 * r + 16].T.reshape(-1) for r in range(8)]).astype(np.int64)
    return lists[np.arange(k) % 512 // 64]


def pack_weight(w):
    k, n = w.shape
    w = f64(np.asarray(w, np.float32).astype(ml_dtypes.bfloat16)).reshape(k // 32, 32, n)
    amax = np.abs(w).max(1)
    byte = np.clip(np.where(amax > 0, np.frexp(amax)[1] - 1 + 127 - 7, 1), 1, 254)
    scaled = (w * np.exp2(127.0 - byte)[:, None, :]).reshape(k, n).astype(np.float32)
    words = np.ascontiguousarray(scaled.reshape(k // 512, 128, 4, n).transpose(0, 1, 3, 2)).astype(ml_dtypes.float8_e4m3fn).view(np.uint8)
    return words, np.ascontiguousarray(byte.astype(np.uint8).reshape(k // 512, 16, n))


def unpack_weight(words, scales):
    g, p, n, _ = words.shape
    vals = np.ascontiguousarray(words).view(ml_dtypes.float8_e4m3fn).astype(np.float64) * np.repeat(np.exp2(scales.astype(np.float64) - 127.0), 8, axis=1)[..., None]
    return vals.transpose(0, 1, 3, 2).reshape(g * 512, n)


def relu(v):
    return np.maximum(v, 0.0)

def planes(y):
    n, m = y.shape
    v = y.astype(np.float32).astype(ml_dtypes.bfloat16).astype(np.float64).reshape(n // 32, 32, m)
    top = np.abs(v).max(1)
    byte = np.clip(np.where(top > 0, np.frexp(top)[1] - 1 + 127 - 7, 1), 1, 254)
    codes = (v * np.exp2(127.0 - byte)[:, None, :]).reshape(n, m).astype(np.float32).astype(ml_dtypes.float8_e4m3fn).view(np.uint8)
    words = codes.reshape(n // 512, 128, 4, m).transpose(0, 1, 3, 2)
    return np.ascontiguousarray(words), np.ascontiguousarray(byte.astype(np.uint8).reshape(n // 512, 16, m))


K, T, S, G, H, W, C, U = 512, 1024, 512, 2048, 512, 256, 512, 1024


def setup_inputs():
    n = np.random.standard_normal
    s = mx_kscale(K)[:, None]
    packed_xT = pack_weight(n((K, T)) * s)
    packed_dT = pack_weight(n((K, G)) / s)
    perm = np.stack([np.random.permutation(S) for _ in range(8)])
    return {
        "x_words": packed_xT[0],
        "x_scales": packed_xT[1],
        "d_words": packed_dT[0],
        "d_scales": packed_dT[1],
        "gs": (np.random.uniform(0.5, 1.5, (K, 1)) / s).astype(np.float32),
        "offs": striped8(np.random.randint(0, T, (8, S))),
        "k1": striped8(np.random.randint(0, G, (8, H))),
        "n1": striped8(perm[:, :W]),
        "n2": striped8(perm[:, W:]),
        "n3": striped8(np.stack([np.random.permutation(S) for _ in range(8)])),
        "cand": striped(np.random.permutation(T)[:C]),
        "n4": striped8(np.stack([np.random.permutation(U)[:S] for _ in range(8)])),
        "n5": striped8(np.stack([np.random.permutation(S) for _ in range(8)])),
    }


def reference(x_words, x_scales, d_words, d_scales, gs, offs, k1, n1, n2, n3, cand, n4, n5):
    x_cand = unpack_weight(x_words, x_scales)[:, unstriped(cand)]
    d_k1 = unpack_weight(d_words, d_scales)[np.arange(K)[:, None], runs(k1, K)]
    xq = unpack_weight(x_words, x_scales)[np.arange(K)[:, None], runs(offs, K)]
    h = 0.0625 * (d_k1.T @ xq)
    pa = h[np.arange(H)[:, None], runs(n1, H)]
    pb = h[np.arange(H)[:, None], runs(n2, H)]
    rb = np.minimum(pa, pb)
    ra = np.maximum(pa, pb)
    ds = np.zeros((H, S))
    ds[np.arange(H)[:, None], runs(n1, H)] = ra
    dt = ds.copy()
    dt[np.arange(H)[:, None], runs(n2, H)] = rb
    z = f64(gs) * (dt - (dt[np.arange(H)[:, None], runs(n3, H)]))
    s = 0.0625 * ((x_cand.T @ mxq(z, 0, "e4m3")))
    nw = s - (relu(s[np.arange(C)[:, None], runs(n5, C)]))
    out = np.zeros((C, U))
    out[np.arange(C)[:, None], runs(n4, C)] = nw
    return (out,) + planes(out)

@@ -1,0 +1,220 @@
+from contextlib import ExitStack
+
+import concourse.mybir as mybir
+
+K, T, S, G, H, W, C, U = 512, 1024, 512, 2048, 512, 256, 512, 1024
+FLOPS = 2 * K * H * S + 2 * K * C * S
+
+F32 = mybir.dt.float32
+BF16 = mybir.dt.bfloat16
+I32 = mybir.dt.int32
+U32 = mybir.dt.uint32
+U16 = mybir.dt.uint16
+U8 = mybir.dt.uint8
+FP8X4 = mybir.dt.float8_e4m3fn_x4
+ALU = mybir.AluOpType
+ACT = mybir.ActivationFunctionType
+
+P = 128
+PACK = 4
+HALF = 256
+CHUNK = 256
+SIXTEENTH = 0.0625
+
+
+def tile_picked_hpqcorddpagez_none_po_kernel(
+    tc, x_words, x_scales, d_words, d_scales, gs, offs, k1, n1, n2, n3, cand, n4, n5, out_0, out_1, out_2
+):
+    nc = tc.nc
+    with ExitStack() as ctx:
+        keep = ctx.enter_context(tc.tile_pool(name="keep", bufs=1))
+        psum = ctx.enter_context(tc.psum_pool(name="psum", bufs=1))
+
+        def new(shape, dtype, name, tag=""):
+            return keep.tile(shape, dtype, name=name, tag=tag or name, align_bytes=64)
+
+        def load_list(ap, name):
+            tile = keep.tile([P, ap.shape[1]], U16, name=name)
+            nc.sync.dma_start(tile[:], ap)
+            return tile
+
+        def dealt(ap):
+            return ap.rearrange("p (t m) -> p m t", t=PACK)
+
+        def in_order(ap):
+            return ap.rearrange("p (m t) -> p m t", t=PACK)
+
+        d_byte_table = new([P, G], U8, "d_byte_table")
+        x_byte_table = new([P, T], U8, "x_byte_table")
+        c_byte_table = new([P, T], U8, "c_byte_table")
+        for table in (d_byte_table, x_byte_table, c_byte_table):
+            nc.vector.memset(table[:].bitcast(I32), 0)
+        k1_l = load_list(k1, "k1_l")
+        d_rows = d_scales[0].bitcast(I32)
+        x_rows = x_scales[0].bitcast(I32)
+        for e in range(2):
+            nc.scalar.dma_start(d_byte_table[e:P:16, :].bitcast(I32), d_rows[e:16:2, :])
+        offs_l = load_list(offs, "offs_l")
+        for e in range(2):
+            nc.scalar.dma_start(x_byte_table[e:P:16, :].bitcast(I32), x_rows[e:16:2, :])
+        x_word_table = new([P, T], U32, "x_word_table")
+        nc.sync.dma_start(x_word_table[:].bitcast(I32), x_words[0].rearrange("p n t -> p (n t)").bitcast(I32))
+        d_word_table = new([P, G], U32, "d_word_table")
+        nc.sync.dma_start(d_word_table[:].bitcast(I32), d_words[0].rearrange("p n t -> p (n t)").bitcast(I32))
+        gains = new([P, PACK], F32, "gains")
+        nc.gpsimd.dma_start(gains[:], gs.rearrange("(p t) o -> p (t o)", t=PACK))
+        for r in range(4):
+            nc.gpsimd.dma_start(c_byte_table[r:P:32, :].bitcast(I32), x_rows[r:16:4, :])
+        n1_l = load_list(n1, "n1_l")
+        n2_l = load_list(n2, "n2_l")
+        cand_l = load_list(cand, "cand_l")
+        n3_l = load_list(n3, "n3_l")
+        n5_l = load_list(n5, "n5_l")
+        n4_l = load_list(n4, "n4_l")
+
+        def cleared_page(t, tag=""):
+            page = new([P, U], F32, f"page{t}", tag)
+            nc.vector.memset(page[:], 0.0)
+            return page
+
+        pages = [cleared_page(t) for t in range(2)]
+
+        def place_rows(picked, name):
+            plane = new([P, 512], U8, name)
+            nc.vector.tensor_copy(plane[:].bitcast(I32), picked[:].bitcast(I32))
+            for e, queue in enumerate((nc.sync, nc.scalar)):
+                queue.dma_start(plane[2 + e : P : 32, :].bitcast(I32), picked[16 + e : P : 32, :].bitcast(I32))
+            return plane
+
+        d_bytes = new([P, H], U8, "d_bytes")
+        nc.vector.tensor_copy(d_bytes[:], d_byte_table[:].indirect(k1_l[:]))
+        x_bytes = new([P, S], U8, "x_bytes")
+        d_bytes_dealt = new([P, H], U8, "d_bytes_dealt")
+        nc.vector.tensor_copy(dealt(d_bytes_dealt[:]), in_order(d_bytes[:]))
+        nc.vector.tensor_copy(x_bytes[:], x_byte_table[:].indirect(offs_l[:]))
+        d_plane = place_rows(d_bytes_dealt, "d_plane")
+        x_plane = place_rows(x_bytes, "x_plane")
+        x_codes = new([P, S], U32, "x_codes")
+        nc.vector.tensor_copy(x_codes[:], x_word_table[:].indirect(offs_l[:]))
+        d_picked = new([P, H], U32, "d_picked")
+        nc.vector.tensor_copy(d_picked[:], d_word_table[:].indirect(k1_l[:]))
+        d_codes = new([P, H], U32, "d_codes")
+        nc.vector.tensor_copy(dealt(d_codes[:]), in_order(d_picked[:]))
+        c_codes = new([P, C], U32, "c_codes")
+        nc.vector.tensor_copy(dealt(c_codes[:]), x_word_table[:].indirect(cand_l[:]))
+        c_plane = new([P, C], U8, "c_plane")
+        nc.vector.tensor_copy(dealt(c_plane[:]), c_byte_table[:].indirect(cand_l[:]))
+
+        gain_rows = [new([P, W], F32, f"gain_rows{t}") for t in range(PACK)]
+        for t in range(PACK):
+            nc.scalar.activation(gain_rows[t][:], gains[:, t : t + 1].to_broadcast([P, W]), ACT.Copy)
+
+        pa, pb = [], []
+        for t in range(PACK):
+            cols = slice(t * P, (t + 1) * P)
+            bank = psum.tile([P, S], F32, name=f"h_bank{t}")
+            nc.tensor.matmul_mx(
+                out=bank[:], lhsT=d_codes[:, cols].bitcast(FP8X4), lhsT_scale=d_plane[:, cols],
+                rhs=x_codes[:].bitcast(FP8X4), rhs_scale=x_plane[:], start=True, stop=True,
+            )
+            h = new([P, S], F32, f"h{t}")
+            nc.scalar.activation(h[:], bank[:], ACT.Copy, scale=SIXTEENTH)
+            pa.append(new([P, W], F32, f"pa{t}"))
+            pb.append(new([P, W], F32, f"pb{t}"))
+            nc.scalar.activation(pa[t][:], h[:].indirect(n1_l[:]), ACT.Copy)
+            if t == 0:
+                nc.vector.tensor_copy(pb[t][:], h[:].indirect(n2_l[:]))
+            else:
+                nc.scalar.activation(pb[t][:], h[:].indirect(n2_l[:]), ACT.Copy)
+
+        dt, far = [], []
+        for t in range(PACK):
+            ra = new([P, W], F32, f"ra{t}")
+            rb = new([P, W], F32, f"rb{t}")
+            nc.vector.tensor_tensor(ra[:], pa[t][:], pb[t][:], ALU.max)
+            nc.vector.tensor_tensor(rb[:], pa[t][:], pb[t][:], ALU.min)
+            dt.append(new([P, S], F32, f"dt{t}"))
+            nc.vector.tensor_tensor(dt[t][:].indirect(n1_l[:]), ra[:], gain_rows[t][:], ALU.mult)
+            nc.vector.tensor_tensor(dt[t][:].indirect(n2_l[:]), rb[:], gain_rows[t][:], ALU.mult)
+            far.append(new([P, S], F32, f"far{t}"))
+            for a in range(2):
+                nc.scalar.activation(
+                    far[t][:, a * HALF : (a + 1) * HALF], dt[t][:].indirect(n3_l[:, a * 16 : (a + 1) * 16]), ACT.Copy
+                )
+
+        z_pairs = [new([P, 2, HALF, 2], BF16, f"z_pairs{a}") for a in range(2)]
+        for t in range(PACK):
+            for a in range(2):
+                cols = slice(a * HALF, (a + 1) * HALF)
+                nc.vector.tensor_tensor(z_pairs[a][:, t // 2, :, t % 2], dt[t][:, cols], far[t][:, cols], ALU.subtract)
+        z_codes = new([P, S], U32, "z_codes")
+        z_plane = new([P, S], U8, "z_plane")
+        z_grouped = [new([P, HALF * PACK], BF16, f"z_grouped{a}") for a in range(2)]
+        for a in range(2):
+            nc.vector.tensor_copy(
+                z_grouped[a][:].bitcast(I32).rearrange("p (c u) -> p c u", u=2),
+                z_pairs[a][:].rearrange("p u c e -> p u (c e)").bitcast(I32).rearrange("p u c -> p c u"),
+            )
+        for a in range(2):
+            cols = slice(a * HALF, (a + 1) * HALF)
+            nc.vector.quantize_mx(out=z_codes[:, cols].bitcast(FP8X4), scales=z_plane[:, cols], in_=z_grouped[a][:])
+
+        pages += [cleared_page(2 + a, f"z_grouped{a}") for a in range(2)]
+        out_rows = out_0.rearrange("(p t) c -> p t c", t=PACK)
+        n_chunks = U // CHUNK
+        page_pairs = [new([P, 2, CHUNK, 2], BF16, f"page_pairs{k}") for k in range(n_chunks)]
+        scores, minus = [], []
+        for t in range(PACK):
+            cols = slice(t * P, (t + 1) * P)
+            bank = psum.tile([P, S], F32, name=f"s_bank{t}")
+            nc.tensor.matmul_mx(
+                out=bank[:], lhsT=c_codes[:, cols].bitcast(FP8X4), lhsT_scale=c_plane[:, cols],
+                rhs=z_codes[:].bitcast(FP8X4), rhs_scale=z_plane[:], start=True, stop=True,
+            )
+            positive = new([P, S], F32, f"positive{t}")
+            nc.scalar.activation(positive[:], bank[:], ACT.Relu, scale=SIXTEENTH)
+            scores.append(new([P, S], F32, f"scores{t}"))
+            minus.append(new([P, S], F32, f"minus{t}"))
+            if t == 0:
+                nc.vector.tensor_scalar(scores[t][:], bank[:], SIXTEENTH, None, ALU.mult)
+            for a in range(2):
+                nc.scalar.activation(
+                    minus[t][:, a * HALF : (a + 1) * HALF], positive[:].indirect(n5_l[:, a * 16 : (a + 1) * 16]),
+                    ACT.Copy, scale=-1.0,
+                )
+            if t > 0:
+                nc.scalar.activation(scores[t][:], bank[:], ACT.Copy, scale=SIXTEENTH)
+        for t in range(PACK):
+            for a in range(2):
+                cols = slice(a * HALF, (a + 1) * HALF)
+                nc.vector.tensor_tensor(
+                    pages[t][:].indirect(n4_l[:, a * 16 : (a + 1) * 16]), scores[t][:, cols], minus[t][:, cols], ALU.add
+                )
+            nc.sync.dma_start(out_rows[:, t, :], pages[t][:])
+            for k in range(n_chunks):
+                nc.scalar.activation(page_pairs[k][:, t // 2, :, t % 2], pages[t][:, k * CHUNK : (k + 1) * CHUNK], ACT.Copy)
+
+        y_codes = new([P, U], U32, "y_codes")
+        y_plane = new([P, U], U8, "y_plane")
+        y_grouped = [new([P, CHUNK * PACK], BF16, f"y_grouped{k}") for k in range(n_chunks)]
+        out_words = out_1[0].rearrange("p n t -> p (n t)").bitcast(I32)
+        out_bytes = out_2[0].bitcast(I32)
+
+        def regroup(k):
+            nc.vector.tensor_copy(
+                y_grouped[k][:].bitcast(I32).rearrange("p (c u) -> p c u", u=2),
+                page_pairs[k][:].rearrange("p u c e -> p u (c e)").bitcast(I32).rearrange("p u c -> p c u"),
+            )
+
+        regroup(0)
+        for k in range(n_chunks):
+            if k + 1 < n_chunks:
+                regroup(k + 1)
+            cols = slice(k * CHUNK, (k + 1) * CHUNK)
+            nc.vector.quantize_mx(out=y_codes[:, cols].bitcast(FP8X4), scales=y_plane[:, cols], in_=y_grouped[k][:])
+            if k % 2 == 1:
+                both = slice((k - 1) * CHUNK, (k + 1) * CHUNK)
+                nc.sync.dma_start(out_words[:, both], y_codes[:, both].bitcast(I32))
+        for q in range(4):
+            queue = nc.scalar if q % 2 else nc.sync
+            queue.dma_start(out_bytes[4 * q : 4 * q + 4, :], y_plane[32 * q : 32 * q + 4, :].bitcast(I32))

@@ -18,7 +18,8 @@ ACT = mybir.ActivationFunctionType
 P = 128
 PACK = 4
 HALF = 256
-CHUNK = 256
+RUN = 4
+SCALAR_COLS = 384
 SIXTEENTH = 0.0625
 
 
@@ -44,27 +45,30 @@ def tile_picked_hpqcorddpagez_none_po_kernel(
         def in_order(ap):
             return ap.rearrange("p (m t) -> p m t", t=PACK)
 
+        def place_rows(plane, rows, queues):
+            for q in range(4):
+                queues[q % 2].dma_start(
+                    plane[32 * q : 32 * q + 4, :].bitcast(I32), rows[32 * q : 32 * q + 32 : 8, :].bitcast(I32)
+                )
+
         d_byte_table = new([P, G], U8, "d_byte_table")
         x_byte_table = new([P, T], U8, "x_byte_table")
-        c_byte_table = new([P, T], U8, "c_byte_table")
-        for table in (d_byte_table, x_byte_table, c_byte_table):
-            nc.vector.memset(table[:].bitcast(I32), 0)
+        planes = new([P, H + S], U8, "planes")
+        nc.vector.memset(planes[:].bitcast(I32), 0)
+        c_plane = new([P, C], U8, "c_plane")
+        nc.vector.memset(c_plane[:].bitcast(I32), 0)
         k1_l = load_list(k1, "k1_l")
         d_rows = d_scales[0].bitcast(I32)
         x_rows = x_scales[0].bitcast(I32)
-        for e in range(2):
-            nc.scalar.dma_start(d_byte_table[e:P:16, :].bitcast(I32), d_rows[e:16:2, :])
+        nc.scalar.dma_start(d_byte_table[:].bitcast(I32), d_rows.unsqueeze(1).broadcast_to([16, 8, G // 4]))
         offs_l = load_list(offs, "offs_l")
-        for e in range(2):
-            nc.scalar.dma_start(x_byte_table[e:P:16, :].bitcast(I32), x_rows[e:16:2, :])
-        x_word_table = new([P, T], U32, "x_word_table")
-        nc.sync.dma_start(x_word_table[:].bitcast(I32), x_words[0].rearrange("p n t -> p (n t)").bitcast(I32))
+        nc.scalar.dma_start(x_byte_table[:].bitcast(I32), x_rows.unsqueeze(1).broadcast_to([16, 8, T // 4]))
         d_word_table = new([P, G], U32, "d_word_table")
         nc.sync.dma_start(d_word_table[:].bitcast(I32), d_words[0].rearrange("p n t -> p (n t)").bitcast(I32))
+        x_word_table = new([P, T], U32, "x_word_table")
+        nc.sync.dma_start(x_word_table[:].bitcast(I32), x_words[0].rearrange("p n t -> p (n t)").bitcast(I32))
         gains = new([P, PACK], F32, "gains")
         nc.gpsimd.dma_start(gains[:], gs.rearrange("(p t) o -> p (t o)", t=PACK))
-        for r in range(4):
-            nc.gpsimd.dma_start(c_byte_table[r:P:32, :].bitcast(I32), x_rows[r:16:4, :])
         n1_l = load_list(n1, "n1_l")
         n2_l = load_list(n2, "n2_l")
         cand_l = load_list(cand, "cand_l")
@@ -74,36 +78,31 @@ def tile_picked_hpqcorddpagez_none_po_kernel(
 
         def cleared_page(t, tag=""):
             page = new([P, U], F32, f"page{t}", tag)
-            nc.vector.memset(page[:], 0.0)
+            nc.gpsimd.memset(page[:], 0.0)
             return page
 
-        pages = [cleared_page(t) for t in range(2)]
-
-        def place_rows(picked, name):
-            plane = new([P, 512], U8, name)
-            nc.vector.tensor_copy(plane[:].bitcast(I32), picked[:].bitcast(I32))
-            for e, queue in enumerate((nc.sync, nc.scalar)):
-                queue.dma_start(plane[2 + e : P : 32, :].bitcast(I32), picked[16 + e : P : 32, :].bitcast(I32))
-            return plane
+        pages = []
 
         d_bytes = new([P, H], U8, "d_bytes")
         nc.vector.tensor_copy(d_bytes[:], d_byte_table[:].indirect(k1_l[:]))
         x_bytes = new([P, S], U8, "x_bytes")
-        d_bytes_dealt = new([P, H], U8, "d_bytes_dealt")
-        nc.vector.tensor_copy(dealt(d_bytes_dealt[:]), in_order(d_bytes[:]))
         nc.vector.tensor_copy(x_bytes[:], x_byte_table[:].indirect(offs_l[:]))
-        d_plane = place_rows(d_bytes_dealt, "d_plane")
-        x_plane = place_rows(x_bytes, "x_plane")
-        x_codes = new([P, S], U32, "x_codes")
-        nc.vector.tensor_copy(x_codes[:], x_word_table[:].indirect(offs_l[:]))
-        d_picked = new([P, H], U32, "d_picked")
+        picked = new([P, H + S], U8, "picked")
+        nc.vector.tensor_copy(dealt(picked[:, :H]), in_order(d_bytes[:]))
+        nc.vector.tensor_copy(picked[:, H:].bitcast(I32), x_bytes[:].bitcast(I32))
+        place_rows(planes, picked, (nc.sync, nc.scalar))
+        d_plane, x_plane = planes[:, :H], planes[:, H:]
+        d_picked = new([P, H], U32, "d_picked", "d_bytes")
         nc.vector.tensor_copy(d_picked[:], d_word_table[:].indirect(k1_l[:]))
+        x_codes = new([P, S], U32, "x_codes", "x_bytes")
+        nc.vector.tensor_copy(x_codes[:], x_word_table[:].indirect(offs_l[:]))
         d_codes = new([P, H], U32, "d_codes")
         nc.vector.tensor_copy(dealt(d_codes[:]), in_order(d_picked[:]))
-        c_codes = new([P, C], U32, "c_codes")
+        c_codes = new([P, C], U32, "c_codes", "d_bytes")
         nc.vector.tensor_copy(dealt(c_codes[:]), x_word_table[:].indirect(cand_l[:]))
-        c_plane = new([P, C], U8, "c_plane")
-        nc.vector.tensor_copy(dealt(c_plane[:]), c_byte_table[:].indirect(cand_l[:]))
+        c_bytes = new([P, C], U8, "c_bytes", "x_word_table")
+        nc.vector.tensor_copy(dealt(c_bytes[:]), x_byte_table[:].indirect(cand_l[:]))
+        place_rows(c_plane, c_bytes, (nc.sync, nc.sync))
 
         gain_rows = [new([P, W], F32, f"gain_rows{t}") for t in range(PACK)]
         for t in range(PACK):
@@ -115,17 +114,14 @@ def tile_picked_hpqcorddpagez_none_po_kernel(
             bank = psum.tile([P, S], F32, name=f"h_bank{t}")
             nc.tensor.matmul_mx(
                 out=bank[:], lhsT=d_codes[:, cols].bitcast(FP8X4), lhsT_scale=d_plane[:, cols],
-                rhs=x_codes[:].bitcast(FP8X4), rhs_scale=x_plane[:], start=True, stop=True,
+                rhs=x_codes[:].bitcast(FP8X4), rhs_scale=x_plane, start=True, stop=True,
             )
             h = new([P, S], F32, f"h{t}")
             nc.scalar.activation(h[:], bank[:], ACT.Copy, scale=SIXTEENTH)
             pa.append(new([P, W], F32, f"pa{t}"))
             pb.append(new([P, W], F32, f"pb{t}"))
             nc.scalar.activation(pa[t][:], h[:].indirect(n1_l[:]), ACT.Copy)
-            if t == 0:
-                nc.vector.tensor_copy(pb[t][:], h[:].indirect(n2_l[:]))
-            else:
-                nc.scalar.activation(pb[t][:], h[:].indirect(n2_l[:]), ACT.Copy)
+            nc.scalar.activation(pb[t][:], h[:].indirect(n2_l[:]), ACT.Copy)
 
         dt, far = [], []
         for t in range(PACK):
@@ -136,85 +132,99 @@ def tile_picked_hpqcorddpagez_none_po_kernel(
             dt.append(new([P, S], F32, f"dt{t}"))
             nc.vector.tensor_tensor(dt[t][:].indirect(n1_l[:]), ra[:], gain_rows[t][:], ALU.mult)
             nc.vector.tensor_tensor(dt[t][:].indirect(n2_l[:]), rb[:], gain_rows[t][:], ALU.mult)
+            pages.append(cleared_page(t, f"ra{t}"))
             far.append(new([P, S], F32, f"far{t}"))
             for a in range(2):
                 nc.scalar.activation(
                     far[t][:, a * HALF : (a + 1) * HALF], dt[t][:].indirect(n3_l[:, a * 16 : (a + 1) * 16]), ACT.Copy
                 )
 
-        z_pairs = [new([P, 2, HALF, 2], BF16, f"z_pairs{a}") for a in range(2)]
+        def interleave(copy, grouped, rows):
+            copy(
+                grouped.rearrange("p (c i t) -> p c t i", i=RUN, t=PACK),
+                rows.rearrange("p t (c i) -> p c t i", i=RUN),
+            )
+
+        z_rows = [new([P, PACK, HALF], BF16, f"z_rows{a}") for a in range(2)]
         for t in range(PACK):
             for a in range(2):
                 cols = slice(a * HALF, (a + 1) * HALF)
-                nc.vector.tensor_tensor(z_pairs[a][:, t // 2, :, t % 2], dt[t][:, cols], far[t][:, cols], ALU.subtract)
+                nc.vector.tensor_tensor(z_rows[a][:, t, :], dt[t][:, cols], far[t][:, cols], ALU.subtract)
         z_codes = new([P, S], U32, "z_codes")
         z_plane = new([P, S], U8, "z_plane")
         z_grouped = [new([P, HALF * PACK], BF16, f"z_grouped{a}") for a in range(2)]
-        for a in range(2):
-            nc.vector.tensor_copy(
-                z_grouped[a][:].bitcast(I32).rearrange("p (c u) -> p c u", u=2),
-                z_pairs[a][:].rearrange("p u c e -> p u (c e)").bitcast(I32).rearrange("p u c -> p c u"),
-            )
-        for a in range(2):
+        interleave(nc.scalar.copy, z_grouped[0][:], z_rows[0][:])
+        interleave(nc.vector.tensor_copy, z_grouped[1][:], z_rows[1][:])
+        for a in (1, 0):
             cols = slice(a * HALF, (a + 1) * HALF)
             nc.vector.quantize_mx(out=z_codes[:, cols].bitcast(FP8X4), scales=z_plane[:, cols], in_=z_grouped[a][:])
 
-        pages += [cleared_page(2 + a, f"z_grouped{a}") for a in range(2)]
         out_rows = out_0.rearrange("(p t) c -> p t c", t=PACK)
-        n_chunks = U // CHUNK
-        page_pairs = [new([P, 2, CHUNK, 2], BF16, f"page_pairs{k}") for k in range(n_chunks)]
-        scores, minus = [], []
-        for t in range(PACK):
-            cols = slice(t * P, (t + 1) * P)
-            bank = psum.tile([P, S], F32, name=f"s_bank{t}")
+
+        def score(t, cols, bank):
+            rows = slice(t * P, (t + 1) * P)
             nc.tensor.matmul_mx(
-                out=bank[:], lhsT=c_codes[:, cols].bitcast(FP8X4), lhsT_scale=c_plane[:, cols],
-                rhs=z_codes[:].bitcast(FP8X4), rhs_scale=z_plane[:], start=True, stop=True,
+                out=bank, lhsT=c_codes[:, rows].bitcast(FP8X4), lhsT_scale=c_plane[:, rows],
+                rhs=z_codes[:, cols].bitcast(FP8X4), rhs_scale=z_plane[:, cols], start=True, stop=True,
             )
-            positive = new([P, S], F32, f"positive{t}")
-            nc.scalar.activation(positive[:], bank[:], ACT.Relu, scale=SIXTEENTH)
-            scores.append(new([P, S], F32, f"scores{t}"))
-            minus.append(new([P, S], F32, f"minus{t}"))
-            if t == 0:
-                nc.vector.tensor_scalar(scores[t][:], bank[:], SIXTEENTH, None, ALU.mult)
-            for a in range(2):
-                nc.scalar.activation(
-                    minus[t][:, a * HALF : (a + 1) * HALF], positive[:].indirect(n5_l[:, a * 16 : (a + 1) * 16]),
-                    ACT.Copy, scale=-1.0,
-                )
-            if t > 0:
-                nc.scalar.activation(scores[t][:], bank[:], ACT.Copy, scale=SIXTEENTH)
+
+        both = {t: new([P, 2 * S], F32, f"both{t}") for t in range(1, PACK)}
+        scores0 = new([P, S], F32, "scores0")
+        minus = [new([P, S], F32, f"minus{t}") for t in range(PACK)]
+        positive0 = new([P, S], F32, "positive0")
+        for a in (1, 0):
+            cols = slice(a * HALF, (a + 1) * HALF)
+            bank = psum.tile([P, HALF], F32, name=f"first_bank{a}", tag=f"h_bank{a}")
+            score(0, cols, bank[:])
+            nc.scalar.activation(positive0[:, cols], bank[:], ACT.Relu, scale=SIXTEENTH)
+            nc.vector.tensor_scalar(scores0[:, cols], bank[:], SIXTEENTH, None, ALU.mult)
+        for a in range(2):
+            nc.scalar.activation(
+                minus[0][:, a * HALF : (a + 1) * HALF], positive0[:].indirect(n5_l[:, a * 16 : (a + 1) * 16]),
+                ACT.Copy, scale=-1.0,
+            )
+        scores = [scores0[:]]
+        for t in range(1, PACK):
+            bank = psum.tile([P, S], F32, name=f"s_bank{t}")
+            score(t, slice(0, S), bank[:])
+            nc.scalar.activation(both[t][:, :S], bank[:], ACT.Relu, scale=SIXTEENTH)
+            nc.scalar.activation(both[t][:, S:], bank[:], ACT.Copy, scale=SIXTEENTH)
+            nc.scalar.activation(minus[t][:], both[t][:].indirect(n5_l[:]), ACT.Copy, scale=-1.0)
+            scores.append(both[t][:, S:])
+
+        y_rows_s = new([P, PACK, SCALAR_COLS], BF16, "y_rows_s")
+        y_rows_v = new([P, PACK, U - SCALAR_COLS], BF16, "y_rows_v")
         for t in range(PACK):
-            for a in range(2):
-                cols = slice(a * HALF, (a + 1) * HALF)
-                nc.vector.tensor_tensor(
-                    pages[t][:].indirect(n4_l[:, a * 16 : (a + 1) * 16]), scores[t][:, cols], minus[t][:, cols], ALU.add
-                )
+            if t == 0:
+                for a in range(2):
+                    cols = slice(a * HALF, (a + 1) * HALF)
+                    nc.vector.tensor_tensor(
+                        pages[t][:].indirect(n4_l[:, a * 16 : (a + 1) * 16]), scores[t][:, cols], minus[t][:, cols], ALU.add
+                    )
+            else:
+                nc.vector.tensor_tensor(pages[t][:].indirect(n4_l[:]), scores[t], minus[t][:], ALU.add)
             nc.sync.dma_start(out_rows[:, t, :], pages[t][:])
-            for k in range(n_chunks):
-                nc.scalar.activation(page_pairs[k][:, t // 2, :, t % 2], pages[t][:, k * CHUNK : (k + 1) * CHUNK], ACT.Copy)
+            nc.scalar.copy(y_rows_s[:, t, :], pages[t][:, :SCALAR_COLS])
+            if t < PACK - 1:
+                nc.scalar.copy(y_rows_v[:, t, :], pages[t][:, SCALAR_COLS:])
+            else:
+                nc.vector.tensor_copy(y_rows_v[:, t, :], pages[t][:, SCALAR_COLS:])
 
         y_codes = new([P, U], U32, "y_codes")
         y_plane = new([P, U], U8, "y_plane")
-        y_grouped = [new([P, CHUNK * PACK], BF16, f"y_grouped{k}") for k in range(n_chunks)]
         out_words = out_1[0].rearrange("p n t -> p (n t)").bitcast(I32)
         out_bytes = out_2[0].bitcast(I32)
-
-        def regroup(k):
-            nc.vector.tensor_copy(
-                y_grouped[k][:].bitcast(I32).rearrange("p (c u) -> p c u", u=2),
-                page_pairs[k][:].rearrange("p u c e -> p u (c e)").bitcast(I32).rearrange("p u c -> p c u"),
-            )
-
-        regroup(0)
-        for k in range(n_chunks):
-            if k + 1 < n_chunks:
-                regroup(k + 1)
-            cols = slice(k * CHUNK, (k + 1) * CHUNK)
-            nc.vector.quantize_mx(out=y_codes[:, cols].bitcast(FP8X4), scales=y_plane[:, cols], in_=y_grouped[k][:])
-            if k % 2 == 1:
-                both = slice((k - 1) * CHUNK, (k + 1) * CHUNK)
-                nc.sync.dma_start(out_words[:, both], y_codes[:, both].bitcast(I32))
+        pieces = [(SCALAR_COLS, SCALAR_COLS + 512), (SCALAR_COLS + 512, U), (0, SCALAR_COLS)]
+        y_grouped = [new([P, (hi - lo) * PACK], BF16, f"y_grouped{lo}") for lo, hi in pieces]
+        interleave(nc.scalar.copy, y_grouped[2][:], y_rows_s[:])
+        for k in range(2):
+            lo, hi = pieces[k]
+            interleave(nc.vector.tensor_copy, y_grouped[k][:], y_rows_v[:, :, lo - SCALAR_COLS : hi - SCALAR_COLS])
+        for k, (lo, hi) in enumerate(pieces):
+            nc.vector.quantize_mx(out=y_codes[:, lo:hi].bitcast(FP8X4), scales=y_plane[:, lo:hi], in_=y_grouped[k][:])
+            if k == 1:
+                nc.sync.dma_start(out_words[:, SCALAR_COLS:], y_codes[:, SCALAR_COLS:].bitcast(I32))
+        nc.scalar.dma_start(out_words[:, :SCALAR_COLS], y_codes[:, :SCALAR_COLS].bitcast(I32))
         for q in range(4):
             queue = nc.scalar if q % 2 else nc.sync
             queue.dma_start(out_bytes[4 * q : 4 * q + 4, :], y_plane[32 * q : 32 * q + 4, :].bitcast(I32))

@@ -19,7 +19,8 @@ P = 128
 PACK = 4
 HALF = 256
 RUN = 4
-SCALAR_COLS = 384
+Z_SCALAR = 128
+STRIP = 128
 SIXTEENTH = 0.0625
 
 
@@ -57,21 +58,21 @@ def tile_picked_hpqcorddpagez_none_po_kernel(
         nc.vector.memset(planes[:].bitcast(I32), 0)
         c_plane = new([P, C], U8, "c_plane")
         nc.vector.memset(c_plane[:].bitcast(I32), 0)
-        k1_l = load_list(k1, "k1_l")
         d_rows = d_scales[0].bitcast(I32)
         x_rows = x_scales[0].bitcast(I32)
-        nc.scalar.dma_start(d_byte_table[:].bitcast(I32), d_rows.unsqueeze(1).broadcast_to([16, 8, G // 4]))
         offs_l = load_list(offs, "offs_l")
         nc.scalar.dma_start(x_byte_table[:].bitcast(I32), x_rows.unsqueeze(1).broadcast_to([16, 8, T // 4]))
-        d_word_table = new([P, G], U32, "d_word_table")
-        nc.sync.dma_start(d_word_table[:].bitcast(I32), d_words[0].rearrange("p n t -> p (n t)").bitcast(I32))
-        x_word_table = new([P, T], U32, "x_word_table")
-        nc.sync.dma_start(x_word_table[:].bitcast(I32), x_words[0].rearrange("p n t -> p (n t)").bitcast(I32))
-        gains = new([P, PACK], F32, "gains")
-        nc.gpsimd.dma_start(gains[:], gs.rearrange("(p t) o -> p (t o)", t=PACK))
+        k1_l = load_list(k1, "k1_l")
+        nc.scalar.dma_start(d_byte_table[:].bitcast(I32), d_rows.unsqueeze(1).broadcast_to([16, 8, G // 4]))
+        cand_l = load_list(cand, "cand_l")
         n1_l = load_list(n1, "n1_l")
         n2_l = load_list(n2, "n2_l")
-        cand_l = load_list(cand, "cand_l")
+        x_word_table = new([P, T], U32, "x_word_table")
+        nc.sync.dma_start(x_word_table[:].bitcast(I32), x_words[0].rearrange("p n t -> p (n t)").bitcast(I32))
+        d_word_table = new([P, G], U32, "d_word_table")
+        nc.sync.dma_start(d_word_table[:].bitcast(I32), d_words[0].rearrange("p n t -> p (n t)").bitcast(I32))
+        gains = new([P, PACK], F32, "gains")
+        nc.gpsimd.dma_start(gains[:], gs.rearrange("(p t) o -> p (t o)", t=PACK))
         n3_l = load_list(n3, "n3_l")
         n5_l = load_list(n5, "n5_l")
         n4_l = load_list(n4, "n4_l")
@@ -83,22 +84,22 @@ def tile_picked_hpqcorddpagez_none_po_kernel(
 
         pages = []
 
-        d_bytes = new([P, H], U8, "d_bytes")
-        nc.vector.tensor_copy(d_bytes[:], d_byte_table[:].indirect(k1_l[:]))
         x_bytes = new([P, S], U8, "x_bytes")
         nc.vector.tensor_copy(x_bytes[:], x_byte_table[:].indirect(offs_l[:]))
+        d_bytes = new([P, H], U8, "d_bytes")
+        nc.vector.tensor_copy(d_bytes[:], d_byte_table[:].indirect(k1_l[:]))
         picked = new([P, H + S], U8, "picked")
-        nc.vector.tensor_copy(dealt(picked[:, :H]), in_order(d_bytes[:]))
         nc.vector.tensor_copy(picked[:, H:].bitcast(I32), x_bytes[:].bitcast(I32))
+        nc.vector.tensor_copy(dealt(picked[:, :H]), in_order(d_bytes[:]))
         place_rows(planes, picked, (nc.sync, nc.scalar))
         d_plane, x_plane = planes[:, :H], planes[:, H:]
-        d_picked = new([P, H], U32, "d_picked", "d_bytes")
-        nc.vector.tensor_copy(d_picked[:], d_word_table[:].indirect(k1_l[:]))
-        x_codes = new([P, S], U32, "x_codes", "x_bytes")
+        x_codes = new([P, S], U32, "x_codes", "d_bytes")
         nc.vector.tensor_copy(x_codes[:], x_word_table[:].indirect(offs_l[:]))
+        d_picked = new([P, H], U32, "d_picked")
+        nc.vector.tensor_copy(d_picked[:], d_word_table[:].indirect(k1_l[:]))
         d_codes = new([P, H], U32, "d_codes")
         nc.vector.tensor_copy(dealt(d_codes[:]), in_order(d_picked[:]))
-        c_codes = new([P, C], U32, "c_codes", "d_bytes")
+        c_codes = new([P, C], U32, "c_codes", "d_picked")
         nc.vector.tensor_copy(dealt(c_codes[:]), x_word_table[:].indirect(cand_l[:]))
         c_bytes = new([P, C], U8, "c_bytes", "x_word_table")
         nc.vector.tensor_copy(dealt(c_bytes[:]), x_byte_table[:].indirect(cand_l[:]))
@@ -111,13 +112,14 @@ def tile_picked_hpqcorddpagez_none_po_kernel(
         pa, pb = [], []
         for t in range(PACK):
             cols = slice(t * P, (t + 1) * P)
-            bank = psum.tile([P, S], F32, name=f"h_bank{t}")
-            nc.tensor.matmul_mx(
-                out=bank[:], lhsT=d_codes[:, cols].bitcast(FP8X4), lhsT_scale=d_plane[:, cols],
-                rhs=x_codes[:].bitcast(FP8X4), rhs_scale=x_plane, start=True, stop=True,
-            )
             h = new([P, S], F32, f"h{t}")
-            nc.scalar.activation(h[:], bank[:], ACT.Copy, scale=SIXTEENTH)
+            for lo, hi in ((0, HALF), (HALF, S)) if t == 0 else ((0, S),):
+                bank = psum.tile([P, hi - lo], F32, name=f"h_bank{t}_{lo}")
+                nc.tensor.matmul_mx(
+                    out=bank[:], lhsT=d_codes[:, cols].bitcast(FP8X4), lhsT_scale=d_plane[:, cols],
+                    rhs=x_codes[:, lo:hi].bitcast(FP8X4), rhs_scale=x_plane[:, lo:hi], start=True, stop=True,
+                )
+                nc.scalar.activation(h[:, lo:hi], bank[:], ACT.Copy, scale=SIXTEENTH)
             pa.append(new([P, W], F32, f"pa{t}"))
             pb.append(new([P, W], F32, f"pb{t}"))
             nc.scalar.activation(pa[t][:], h[:].indirect(n1_l[:]), ACT.Copy)
@@ -145,16 +147,15 @@ def tile_picked_hpqcorddpagez_none_po_kernel(
                 rows.rearrange("p t (c i) -> p c t i", i=RUN),
             )
 
-        z_rows = [new([P, PACK, HALF], BF16, f"z_rows{a}") for a in range(2)]
+        z_rows = new([P, PACK, S], BF16, "z_rows")
         for t in range(PACK):
-            for a in range(2):
-                cols = slice(a * HALF, (a + 1) * HALF)
-                nc.vector.tensor_tensor(z_rows[a][:, t, :], dt[t][:, cols], far[t][:, cols], ALU.subtract)
+            nc.vector.tensor_tensor(z_rows[:, t, :], dt[t][:], far[t][:], ALU.subtract)
         z_codes = new([P, S], U32, "z_codes")
         z_plane = new([P, S], U8, "z_plane")
         z_grouped = [new([P, HALF * PACK], BF16, f"z_grouped{a}") for a in range(2)]
-        interleave(nc.scalar.copy, z_grouped[0][:], z_rows[0][:])
-        interleave(nc.vector.tensor_copy, z_grouped[1][:], z_rows[1][:])
+        interleave(nc.scalar.copy, z_grouped[0][:, : Z_SCALAR * PACK], z_rows[:, :, :Z_SCALAR])
+        interleave(nc.vector.tensor_copy, z_grouped[1][:], z_rows[:, :, HALF:])
+        interleave(nc.vector.tensor_copy, z_grouped[0][:, Z_SCALAR * PACK :], z_rows[:, :, Z_SCALAR:HALF])
         for a in (1, 0):
             cols = slice(a * HALF, (a + 1) * HALF)
             nc.vector.quantize_mx(out=z_codes[:, cols].bitcast(FP8X4), scales=z_plane[:, cols], in_=z_grouped[a][:])
@@ -174,7 +175,7 @@ def tile_picked_hpqcorddpagez_none_po_kernel(
         positive0 = new([P, S], F32, "positive0")
         for a in (1, 0):
             cols = slice(a * HALF, (a + 1) * HALF)
-            bank = psum.tile([P, HALF], F32, name=f"first_bank{a}", tag=f"h_bank{a}")
+            bank = psum.tile([P, HALF], F32, name=f"first_bank{a}", tag=f"h_bank0_{a * HALF}")
             score(0, cols, bank[:])
             nc.scalar.activation(positive0[:, cols], bank[:], ACT.Relu, scale=SIXTEENTH)
             nc.vector.tensor_scalar(scores0[:, cols], bank[:], SIXTEENTH, None, ALU.mult)
@@ -187,13 +188,19 @@ def tile_picked_hpqcorddpagez_none_po_kernel(
         for t in range(1, PACK):
             bank = psum.tile([P, S], F32, name=f"s_bank{t}")
             score(t, slice(0, S), bank[:])
+            if t == 1:
+                nc.vector.tensor_scalar(both[t][:, S:], bank[:], SIXTEENTH, None, ALU.mult)
             nc.scalar.activation(both[t][:, :S], bank[:], ACT.Relu, scale=SIXTEENTH)
-            nc.scalar.activation(both[t][:, S:], bank[:], ACT.Copy, scale=SIXTEENTH)
+            if t > 1:
+                nc.scalar.activation(both[t][:, S:], bank[:], ACT.Copy, scale=SIXTEENTH)
             nc.scalar.activation(minus[t][:], both[t][:].indirect(n5_l[:]), ACT.Copy, scale=-1.0)
             scores.append(both[t][:, S:])
 
-        y_rows_s = new([P, PACK, SCALAR_COLS], BF16, "y_rows_s")
-        y_rows_v = new([P, PACK, U - SCALAR_COLS], BF16, "y_rows_v")
+        n_strips = U // STRIP - 1
+        groups = [(0, 3), (3, 5), (5, n_strips)]
+        lead_rows = new([P, PACK, STRIP], BF16, "lead_rows")
+        pair_tile = new([P, n_strips * STRIP * PACK], BF16, "pair_tile")
+        y_pairs = pair_tile[:].rearrange("p (k u c e) -> p k u c e", k=n_strips, u=2, e=2)
         for t in range(PACK):
             if t == 0:
                 for a in range(2):
@@ -204,27 +211,35 @@ def tile_picked_hpqcorddpagez_none_po_kernel(
             else:
                 nc.vector.tensor_tensor(pages[t][:].indirect(n4_l[:]), scores[t], minus[t][:], ALU.add)
             nc.sync.dma_start(out_rows[:, t, :], pages[t][:])
-            nc.scalar.copy(y_rows_s[:, t, :], pages[t][:, :SCALAR_COLS])
+            strips = pages[t][:, STRIP:].rearrange("p (k c) -> p k c", c=STRIP)
             if t < PACK - 1:
-                nc.scalar.copy(y_rows_v[:, t, :], pages[t][:, SCALAR_COLS:])
+                nc.scalar.copy(lead_rows[:, t, :], pages[t][:, :STRIP])
+                nc.scalar.copy(y_pairs[:, :, t // 2, :, t % 2], strips)
             else:
-                nc.vector.tensor_copy(y_rows_v[:, t, :], pages[t][:, SCALAR_COLS:])
+                nc.vector.tensor_copy(lead_rows[:, t, :], pages[t][:, :STRIP])
+                for lo, hi in groups:
+                    nc.scalar.copy(y_pairs[:, lo:hi, t // 2, :, t % 2], strips[:, lo:hi, :])
 
         y_codes = new([P, U], U32, "y_codes")
         y_plane = new([P, U], U8, "y_plane")
         out_words = out_1[0].rearrange("p n t -> p (n t)").bitcast(I32)
         out_bytes = out_2[0].bitcast(I32)
-        pieces = [(SCALAR_COLS, SCALAR_COLS + 512), (SCALAR_COLS + 512, U), (0, SCALAR_COLS)]
-        y_grouped = [new([P, (hi - lo) * PACK], BF16, f"y_grouped{lo}") for lo, hi in pieces]
-        interleave(nc.scalar.copy, y_grouped[2][:], y_rows_s[:])
-        for k in range(2):
-            lo, hi = pieces[k]
-            interleave(nc.vector.tensor_copy, y_grouped[k][:], y_rows_v[:, :, lo - SCALAR_COLS : hi - SCALAR_COLS])
-        for k, (lo, hi) in enumerate(pieces):
-            nc.vector.quantize_mx(out=y_codes[:, lo:hi].bitcast(FP8X4), scales=y_plane[:, lo:hi], in_=y_grouped[k][:])
+        edges = [0] + [(hi + 1) * STRIP for lo, hi in groups]
+        for k, (lo, hi) in enumerate(groups):
+            cols = slice(edges[k], edges[k + 1])
+            grouped = new([P, (cols.stop - cols.start) * PACK], BF16, f"y_grouped{k}")
+            lead = STRIP * PACK if k == 0 else 0
+            if k == 0:
+                interleave(nc.vector.tensor_copy, grouped[:, :lead], lead_rows[:])
+            copy, word = (nc.scalar.copy, U32) if hi == n_strips else (nc.vector.tensor_copy, I32)
+            copy(
+                grouped[:, lead:].bitcast(word).rearrange("p (k c u) -> p k c u", c=STRIP, u=2),
+                pair_tile[:, lo * STRIP * PACK : hi * STRIP * PACK].bitcast(word).rearrange("p (k u c) -> p k c u", c=STRIP, u=2),
+            )
+            nc.vector.quantize_mx(out=y_codes[:, cols].bitcast(FP8X4), scales=y_plane[:, cols], in_=grouped[:])
             if k == 1:
-                nc.sync.dma_start(out_words[:, SCALAR_COLS:], y_codes[:, SCALAR_COLS:].bitcast(I32))
-        nc.scalar.dma_start(out_words[:, :SCALAR_COLS], y_codes[:, :SCALAR_COLS].bitcast(I32))
+                nc.sync.dma_start(out_words[:, : cols.stop], y_codes[:, : cols.stop].bitcast(I32))
+        nc.scalar.dma_start(out_words[:, 768:], y_codes[:, 768:].bitcast(I32))
         for q in range(4):
             queue = nc.scalar if q % 2 else nc.sync
             queue.dma_start(out_bytes[4 * q : 4 * q + 4, :], y_plane[32 * q : 32 * q + 4, :].bitcast(I32))

from contextlib import ExitStack

import concourse.mybir as mybir

K, T, S, G, H, W, C, U = 512, 1024, 512, 2048, 512, 256, 512, 1024
FLOPS = 2 * K * H * S + 2 * K * C * S

F32 = mybir.dt.float32
BF16 = mybir.dt.bfloat16
I32 = mybir.dt.int32
U32 = mybir.dt.uint32
U16 = mybir.dt.uint16
U8 = mybir.dt.uint8
FP8X4 = mybir.dt.float8_e4m3fn_x4
ALU = mybir.AluOpType
ACT = mybir.ActivationFunctionType

P = 128
PACK = 4
HALF = 256
RUN = 4
Z_SCALAR = 128
STRIP = 128
SIXTEENTH = 0.0625


def tile_picked_hpqcorddpagez_none_po_kernel(
    tc, x_words, x_scales, d_words, d_scales, gs, offs, k1, n1, n2, n3, cand, n4, n5, out_0, out_1, out_2
):
    nc = tc.nc
    with ExitStack() as ctx:
        keep = ctx.enter_context(tc.tile_pool(name="keep", bufs=1))
        psum = ctx.enter_context(tc.psum_pool(name="psum", bufs=1))

        def new(shape, dtype, name, tag=""):
            return keep.tile(shape, dtype, name=name, tag=tag or name, align_bytes=64)

        def load_list(ap, name):
            tile = keep.tile([P, ap.shape[1]], U16, name=name)
            nc.sync.dma_start(tile[:], ap)
            return tile

        def dealt(ap):
            return ap.rearrange("p (t m) -> p m t", t=PACK)

        def in_order(ap):
            return ap.rearrange("p (m t) -> p m t", t=PACK)

        def place_rows(plane, rows, queues):
            for q in range(4):
                queues[q % 2].dma_start(
                    plane[32 * q : 32 * q + 4, :].bitcast(I32), rows[32 * q : 32 * q + 32 : 8, :].bitcast(I32)
                )

        d_byte_table = new([P, G], U8, "d_byte_table")
        x_byte_table = new([P, T], U8, "x_byte_table")
        planes = new([P, H + S], U8, "planes")
        nc.vector.memset(planes[:].bitcast(I32), 0)
        c_plane = new([P, C], U8, "c_plane")
        nc.vector.memset(c_plane[:].bitcast(I32), 0)
        d_rows = d_scales[0].bitcast(I32)
        x_rows = x_scales[0].bitcast(I32)
        offs_l = load_list(offs, "offs_l")
        nc.scalar.dma_start(x_byte_table[:].bitcast(I32), x_rows.unsqueeze(1).broadcast_to([16, 8, T // 4]))
        k1_l = load_list(k1, "k1_l")
        nc.scalar.dma_start(d_byte_table[:].bitcast(I32), d_rows.unsqueeze(1).broadcast_to([16, 8, G // 4]))
        cand_l = load_list(cand, "cand_l")
        n1_l = load_list(n1, "n1_l")
        n2_l = load_list(n2, "n2_l")
        x_word_table = new([P, T], U32, "x_word_table")
        nc.sync.dma_start(x_word_table[:].bitcast(I32), x_words[0].rearrange("p n t -> p (n t)").bitcast(I32))
        d_word_table = new([P, G], U32, "d_word_table")
        nc.sync.dma_start(d_word_table[:].bitcast(I32), d_words[0].rearrange("p n t -> p (n t)").bitcast(I32))
        gains = new([P, PACK], F32, "gains")
        nc.gpsimd.dma_start(gains[:], gs.rearrange("(p t) o -> p (t o)", t=PACK))
        n3_l = load_list(n3, "n3_l")
        n5_l = load_list(n5, "n5_l")
        n4_l = load_list(n4, "n4_l")

        def cleared_page(t, tag=""):
            page = new([P, U], F32, f"page{t}", tag)
            nc.gpsimd.memset(page[:], 0.0)
            return page

        pages = []

        x_bytes = new([P, S], U8, "x_bytes")
        nc.vector.tensor_copy(x_bytes[:], x_byte_table[:].indirect(offs_l[:]))
        d_bytes = new([P, H], U8, "d_bytes")
        nc.vector.tensor_copy(d_bytes[:], d_byte_table[:].indirect(k1_l[:]))
        picked = new([P, H + S], U8, "picked")
        nc.vector.tensor_copy(picked[:, H:].bitcast(I32), x_bytes[:].bitcast(I32))
        nc.vector.tensor_copy(dealt(picked[:, :H]), in_order(d_bytes[:]))
        place_rows(planes, picked, (nc.sync, nc.scalar))
        d_plane, x_plane = planes[:, :H], planes[:, H:]
        x_codes = new([P, S], U32, "x_codes", "d_bytes")
        nc.vector.tensor_copy(x_codes[:], x_word_table[:].indirect(offs_l[:]))
        d_picked = new([P, H], U32, "d_picked")
        nc.vector.tensor_copy(d_picked[:], d_word_table[:].indirect(k1_l[:]))
        d_codes = new([P, H], U32, "d_codes")
        nc.vector.tensor_copy(dealt(d_codes[:]), in_order(d_picked[:]))
        c_codes = new([P, C], U32, "c_codes", "d_picked")
        nc.vector.tensor_copy(dealt(c_codes[:]), x_word_table[:].indirect(cand_l[:]))
        c_bytes = new([P, C], U8, "c_bytes", "x_word_table")
        nc.vector.tensor_copy(dealt(c_bytes[:]), x_byte_table[:].indirect(cand_l[:]))
        place_rows(c_plane, c_bytes, (nc.sync, nc.sync))

        gain_rows = [new([P, W], F32, f"gain_rows{t}") for t in range(PACK)]
        for t in range(PACK):
            nc.scalar.activation(gain_rows[t][:], gains[:, t : t + 1].to_broadcast([P, W]), ACT.Copy)

        pa, pb = [], []
        for t in range(PACK):
            cols = slice(t * P, (t + 1) * P)
            h = new([P, S], F32, f"h{t}")
            for lo, hi in ((0, HALF), (HALF, S)) if t == 0 else ((0, S),):
                bank = psum.tile([P, hi - lo], F32, name=f"h_bank{t}_{lo}")
                nc.tensor.matmul_mx(
                    out=bank[:], lhsT=d_codes[:, cols].bitcast(FP8X4), lhsT_scale=d_plane[:, cols],
                    rhs=x_codes[:, lo:hi].bitcast(FP8X4), rhs_scale=x_plane[:, lo:hi], start=True, stop=True,
                )
                nc.scalar.activation(h[:, lo:hi], bank[:], ACT.Copy, scale=SIXTEENTH)
            pa.append(new([P, W], F32, f"pa{t}"))
            pb.append(new([P, W], F32, f"pb{t}"))
            nc.scalar.activation(pa[t][:], h[:].indirect(n1_l[:]), ACT.Copy)
            nc.scalar.activation(pb[t][:], h[:].indirect(n2_l[:]), ACT.Copy)

        dt, far = [], []
        for t in range(PACK):
            ra = new([P, W], F32, f"ra{t}")
            rb = new([P, W], F32, f"rb{t}")
            nc.vector.tensor_tensor(ra[:], pa[t][:], pb[t][:], ALU.max)
            nc.vector.tensor_tensor(rb[:], pa[t][:], pb[t][:], ALU.min)
            dt.append(new([P, S], F32, f"dt{t}"))
            nc.vector.tensor_tensor(dt[t][:].indirect(n1_l[:]), ra[:], gain_rows[t][:], ALU.mult)
            nc.vector.tensor_tensor(dt[t][:].indirect(n2_l[:]), rb[:], gain_rows[t][:], ALU.mult)
            pages.append(cleared_page(t, f"ra{t}"))
            far.append(new([P, S], F32, f"far{t}"))
            for a in range(2):
                nc.scalar.activation(
                    far[t][:, a * HALF : (a + 1) * HALF], dt[t][:].indirect(n3_l[:, a * 16 : (a + 1) * 16]), ACT.Copy
                )

        def interleave(copy, grouped, rows):
            copy(
                grouped.rearrange("p (c i t) -> p c t i", i=RUN, t=PACK),
                rows.rearrange("p t (c i) -> p c t i", i=RUN),
            )

        z_rows = new([P, PACK, S], BF16, "z_rows")
        for t in range(PACK):
            nc.vector.tensor_tensor(z_rows[:, t, :], dt[t][:], far[t][:], ALU.subtract)
        z_codes = new([P, S], U32, "z_codes")
        z_plane = new([P, S], U8, "z_plane")
        z_grouped = [new([P, HALF * PACK], BF16, f"z_grouped{a}") for a in range(2)]
        interleave(nc.scalar.copy, z_grouped[0][:, : Z_SCALAR * PACK], z_rows[:, :, :Z_SCALAR])
        interleave(nc.vector.tensor_copy, z_grouped[1][:], z_rows[:, :, HALF:])
        interleave(nc.vector.tensor_copy, z_grouped[0][:, Z_SCALAR * PACK :], z_rows[:, :, Z_SCALAR:HALF])
        for a in (1, 0):
            cols = slice(a * HALF, (a + 1) * HALF)
            nc.vector.quantize_mx(out=z_codes[:, cols].bitcast(FP8X4), scales=z_plane[:, cols], in_=z_grouped[a][:])

        out_rows = out_0.rearrange("(p t) c -> p t c", t=PACK)

        def score(t, cols, bank):
            rows = slice(t * P, (t + 1) * P)
            nc.tensor.matmul_mx(
                out=bank, lhsT=c_codes[:, rows].bitcast(FP8X4), lhsT_scale=c_plane[:, rows],
                rhs=z_codes[:, cols].bitcast(FP8X4), rhs_scale=z_plane[:, cols], start=True, stop=True,
            )

        both = {t: new([P, 2 * S], F32, f"both{t}") for t in range(1, PACK)}
        scores0 = new([P, S], F32, "scores0")
        minus = [new([P, S], F32, f"minus{t}") for t in range(PACK)]
        positive0 = new([P, S], F32, "positive0")
        for a in (1, 0):
            cols = slice(a * HALF, (a + 1) * HALF)
            bank = psum.tile([P, HALF], F32, name=f"first_bank{a}", tag=f"h_bank0_{a * HALF}")
            score(0, cols, bank[:])
            nc.scalar.activation(positive0[:, cols], bank[:], ACT.Relu, scale=SIXTEENTH)
            nc.vector.tensor_scalar(scores0[:, cols], bank[:], SIXTEENTH, None, ALU.mult)
        for a in range(2):
            nc.scalar.activation(
                minus[0][:, a * HALF : (a + 1) * HALF], positive0[:].indirect(n5_l[:, a * 16 : (a + 1) * 16]),
                ACT.Copy, scale=-1.0,
            )
        scores = [scores0[:]]
        for t in range(1, PACK):
            bank = psum.tile([P, S], F32, name=f"s_bank{t}")
            score(t, slice(0, S), bank[:])
            if t == 1:
                nc.vector.tensor_scalar(both[t][:, S:], bank[:], SIXTEENTH, None, ALU.mult)
            nc.scalar.activation(both[t][:, :S], bank[:], ACT.Relu, scale=SIXTEENTH)
            if t > 1:
                nc.scalar.activation(both[t][:, S:], bank[:], ACT.Copy, scale=SIXTEENTH)
            nc.scalar.activation(minus[t][:], both[t][:].indirect(n5_l[:]), ACT.Copy, scale=-1.0)
            scores.append(both[t][:, S:])

        n_strips = U // STRIP - 1
        groups = [(0, 3), (3, 5), (5, n_strips)]
        lead_rows = new([P, PACK, STRIP], BF16, "lead_rows")
        pair_tile = new([P, n_strips * STRIP * PACK], BF16, "pair_tile")
        y_pairs = pair_tile[:].rearrange("p (k u c e) -> p k u c e", k=n_strips, u=2, e=2)
        for t in range(PACK):
            if t == 0:
                for a in range(2):
                    cols = slice(a * HALF, (a + 1) * HALF)
                    nc.vector.tensor_tensor(
                        pages[t][:].indirect(n4_l[:, a * 16 : (a + 1) * 16]), scores[t][:, cols], minus[t][:, cols], ALU.add
                    )
            else:
                nc.vector.tensor_tensor(pages[t][:].indirect(n4_l[:]), scores[t], minus[t][:], ALU.add)
            nc.sync.dma_start(out_rows[:, t, :], pages[t][:])
            strips = pages[t][:, STRIP:].rearrange("p (k c) -> p k c", c=STRIP)
            if t < PACK - 1:
                nc.scalar.copy(lead_rows[:, t, :], pages[t][:, :STRIP])
                nc.scalar.copy(y_pairs[:, :, t // 2, :, t % 2], strips)
            else:
                nc.vector.tensor_copy(lead_rows[:, t, :], pages[t][:, :STRIP])
                for lo, hi in groups:
                    nc.scalar.copy(y_pairs[:, lo:hi, t // 2, :, t % 2], strips[:, lo:hi, :])

        y_codes = new([P, U], U32, "y_codes")
        y_plane = new([P, U], U8, "y_plane")
        out_words = out_1[0].rearrange("p n t -> p (n t)").bitcast(I32)
        out_bytes = out_2[0].bitcast(I32)
        edges = [0] + [(hi + 1) * STRIP for lo, hi in groups]
        for k, (lo, hi) in enumerate(groups):
            cols = slice(edges[k], edges[k + 1])
            grouped = new([P, (cols.stop - cols.start) * PACK], BF16, f"y_grouped{k}")
            lead = STRIP * PACK if k == 0 else 0
            if k == 0:
                interleave(nc.vector.tensor_copy, grouped[:, :lead], lead_rows[:])
            copy, word = (nc.scalar.copy, U32) if hi == n_strips else (nc.vector.tensor_copy, I32)
            copy(
                grouped[:, lead:].bitcast(word).rearrange("p (k c u) -> p k c u", c=STRIP, u=2),
                pair_tile[:, lo * STRIP * PACK : hi * STRIP * PACK].bitcast(word).rearrange("p (k u c) -> p k c u", c=STRIP, u=2),
            )
            nc.vector.quantize_mx(out=y_codes[:, cols].bitcast(FP8X4), scales=y_plane[:, cols], in_=grouped[:])
            if k == 1:
                nc.sync.dma_start(out_words[:, : cols.stop], y_codes[:, : cols.stop].bitcast(I32))
        nc.scalar.dma_start(out_words[:, 768:], y_codes[:, 768:].bitcast(I32))
        for q in range(4):
            queue = nc.scalar if q % 2 else nc.sync
            queue.dma_start(out_bytes[4 * q : 4 * q + 4, :], y_plane[32 * q : 32 * q + 4, :].bitcast(I32))
